import numpy as np
import ml_dtypes


def mxq(x, axis, fmt="e4m3"):
    dtype, down = {"e4m3": (ml_dtypes.float8_e4m3fn, 7), "e5m2": (ml_dtypes.float8_e5m2, 14)}[fmt]
    v = np.moveaxis(np.asarray(x, np.float32).astype(ml_dtypes.bfloat16).astype(np.float64), axis, -1)
    blocks = v.reshape(v.shape[:-1] + (-1, 32))
    amax = np.abs(blocks).max(-1, keepdims=True)
    byte = np.maximum(np.where(amax > 0, np.frexp(amax)[1] - 1 + 127, 0) - down, 1)
    scale = np.exp2(byte - 127.0)
    codes = (blocks / scale).astype(np.float32).astype(dtype).astype(np.float64)
    return np.moveaxis((codes * scale).reshape(v.shape), -1, axis)


WIDE = False


def mx_kscale(k):
    if not WIDE:
        return np.ones(k)
    levels = np.array([10, -10, 5, -5, 0])
    if k % 512:
        return np.exp2(np.random.permutation(np.resize(levels, k // 32))).repeat(32)
    a = np.empty((k // 512, 16))
    for p in range(k // 512):
        a[p, :8] = np.random.permutation(np.resize(levels, 8))
        for g in range(8):
            far = levels[np.abs(levels - a[p, g]) >= 10]
            a[p, g + 8] = far[np.random.randint(len(far))]
    return np.exp2(a.ravel()).repeat(32)


def f64(x):
    return np.asarray(x).astype(np.float64)


def striped(idx):
    return np.tile(idx.reshape(-1, 16).T, (8, 1)).astype(np.uint16)


def unstriped(offs):
    return offs[:16].T.reshape(-1).astype(np.int64)


def striped8(idx):
    return np.concatenate([x.reshape(-1, 16).T for x in idx]).astype(np.uint16)


def runs(offs, k):
    lists = np.stack([offs[16 * r : 16 * r + 16].T.reshape(-1) for r in range(8)]).astype(np.int64)
    return lists[np.arange(k) % 512 // 64]


def pack_weight(w):
    k, n = w.shape
    w = f64(np.asarray(w, np.float32).astype(ml_dtypes.bfloat16)).reshape(k // 32, 32, n)
    amax = np.abs(w).max(1)
    byte = np.clip(np.where(amax > 0, np.frexp(amax)[1] - 1 + 127 - 7, 1), 1, 254)
    scaled = (w * np.exp2(127.0 - byte)[:, None, :]).reshape(k, n).astype(np.float32)
    words = np.ascontiguousarray(scaled.reshape(k // 512, 128, 4, n).transpose(0, 1, 3, 2)).astype(ml_dtypes.float8_e4m3fn).view(np.uint8)
    return words, np.ascontiguousarray(byte.astype(np.uint8).reshape(k // 512, 16, n))


def unpack_weight(words, scales):
    g, p, n, _ = words.shape
    vals = np.ascontiguousarray(words).view(ml_dtypes.float8_e4m3fn).astype(np.float64) * np.repeat(np.exp2(scales.astype(np.float64) - 127.0), 8, axis=1)[..., None]
    return vals.transpose(0, 1, 3, 2).reshape(g * 512, n)

def planes(y):
    n, m = y.shape
    v = y.astype(np.float32).astype(ml_dtypes.bfloat16).astype(np.float64).reshape(n // 32, 32, m)
    top = np.abs(v).max(1)
    byte = np.clip(np.where(top > 0, np.frexp(top)[1] - 1 + 127 - 7, 1), 1, 254)
    codes = (v * np.exp2(127.0 - byte)[:, None, :]).reshape(n, m).astype(np.float32).astype(ml_dtypes.float8_e4m3fn).view(np.uint8)
    words = codes.reshape(n // 512, 128, 4, m).transpose(0, 1, 3, 2)
    return np.ascontiguousarray(words), np.ascontiguousarray(byte.astype(np.uint8).reshape(n // 512, 16, m))


K, T, S, G, H, W = 512, 1024, 512, 2048, 512, 256


def setup_inputs():
    n = np.random.standard_normal
    s = mx_kscale(K)[:, None]
    packed_xT = pack_weight(n((K, T)) * s)
    packed_dT = pack_weight(n((K, G)) / s)
    perm = np.stack([np.random.permutation(S) for _ in range(8)])
    perm2 = np.stack([np.random.permutation(S) for _ in range(8)])
    perm3 = np.random.permutation(S)
    perm4 = np.random.permutation(S)
    return {
        "x_words": packed_xT[0],
        "x_scales": packed_xT[1],
        "d_words": packed_dT[0],
        "d_scales": packed_dT[1],
        "gs": (np.random.uniform(0.5, 1.5, (K, 1)) * s).astype(np.float32),
        "offs": striped(np.random.permutation(T)[:S]),
        "k1": striped8(np.random.randint(0, G, (8, H))),
        "two": striped(np.random.permutation(T)[:S]),
        "k2": striped8(np.random.randint(0, G, (8, H))),
        "hz": striped8(np.random.randint(0, T, (8, S))),
        "k3": striped8(np.random.randint(0, G, (8, H))),
        "n1": striped8(perm[:, :W]),
        "n2": striped8(perm[:, W:]),
        "n3": striped8(perm2[:, :W]),
        "n4": striped8(perm2[:, W:]),
        "n5": striped8(np.stack([np.random.permutation(S) for _ in range(8)])),
        "k4": striped8(np.random.randint(0, G, (8, H))),
        "k5": striped8(np.random.randint(0, G, (8, H))),
        "duo": striped(np.random.permutation(T)[:S]),
        "n6": striped(perm3[:W]),
        "n7": striped(perm3[W:]),
        "n8": striped(perm4[:W]),
        "n9": striped(perm4[W:]),
    }


def reference(x_words, x_scales, d_words, d_scales, gs, offs, k1, two, k2, hz, k3, n1, n2, n3, n4, n5, k4, k5, duo, n6, n7, n8, n9):
    d_k4 = unpack_weight(d_words, d_scales)[np.arange(K)[:, None], runs(k4, K)]
    d_k1 = unpack_weight(d_words, d_scales)[np.arange(K)[:, None], runs(k1, K)]
    xq = unpack_weight(x_words, x_scales)[:, unstriped(offs)]
    d_k2 = unpack_weight(d_words, d_scales)[np.arange(K)[:, None], runs(k2, K)]
    x_two = unpack_weight(x_words, x_scales)[:, unstriped(two)]
    d_k3 = unpack_weight(d_words, d_scales)[np.arange(K)[:, None], runs(k3, K)]
    x_hz = unpack_weight(x_words, x_scales)[np.arange(K)[:, None], runs(hz, K)]
    h = 0.0625 * (d_k1.T @ xq + d_k2.T @ x_two + d_k3.T @ x_hz)
    pa = h[np.arange(H)[:, None], runs(n1, H)]
    pb = h[np.arange(H)[:, None], runs(n2, H)]
    rb = pa + pb
    ra = np.minimum(pa, pb)
    ua = np.zeros((H, S))
    ua[np.arange(H)[:, None], runs(n3, H)] = ra
    ub = ua.copy()
    ub[np.arange(H)[:, None], runs(n4, H)] = rb
    ds = np.zeros((H, S))
    ds[np.arange(H)[:, None], runs(n5, H)] = ub
    z = f64(gs) * (ub - ds)
    d_k5 = unpack_weight(d_words, d_scales)[np.arange(K)[:, None], runs(k5, K)]
    x_duo = unpack_weight(x_words, x_scales)[:, unstriped(duo)]
    h2 = 0.0625 * ((d_k4.T @ mxq(z, 0, "e4m3") + d_k5.T @ x_duo))
    pa2 = h2[:, unstriped(n6)]
    pb2 = h2[:, unstriped(n7)]
    rb2 = pa2 - pb2
    ra2 = np.maximum(pa2, pb2)
    ua2 = np.zeros((H, S))
    ua2[:, unstriped(n8)] = ra2
    out = ua2.copy()
    out[:, unstriped(n9)] = rb2
    return (out,) + planes(out)

@@ -1,0 +1,210 @@
+from contextlib import ExitStack
+
+import concourse.mybir as mybir
+from concourse.masks import make_identity
+
+F32 = mybir.dt.float32
+BF16 = mybir.dt.bfloat16
+I32 = mybir.dt.int32
+U32 = mybir.dt.uint32
+U16 = mybir.dt.uint16
+U8 = mybir.dt.uint8
+FP8X4 = mybir.dt.float8_e4m3fn_x4
+ALU = mybir.AluOpType
+COPY = mybir.ActivationFunctionType.Copy
+
+P = 128
+PACK = 4
+S = 512
+HALF = S // 2
+T_COLS, G_COLS = 1024, 2048
+SIXTEENTH = 0.0625
+FLOPS = 5 * 2 * 512 * 512 * 512
+
+
+def tile_picked_mtthzmtcpsdcpmx_none_po_kernel(
+    tc, x_words, x_scales, d_words, d_scales, gs, offs, k1, two, k2, hz, k3, n1, n2, n3, n4, n5, k4, k5, duo,
+    n6, n7, n8, n9, out_0, out_1, out_2,
+):
+    nc = tc.nc
+    dram_lists = dict(offs=offs, k1=k1, two=two, k2=k2, hz=hz, k3=k3, n1=n1, n2=n2, n3=n3, n4=n4, n5=n5,
+                      k4=k4, k5=k5, duo=duo, n6=n6, n7=n7, n8=n8, n9=n9)
+
+    with ExitStack() as ctx:
+        held = ctx.enter_context(tc.tile_pool(name="held", bufs=1))
+        sb = ctx.enter_context(tc.tile_pool(name="sb", bufs=1))
+        psum = ctx.enter_context(tc.psum_pool(name="psum", bufs=1))
+
+        def tile(name, shape, dtype, tag=None):
+            return sb.tile(shape, dtype, name=name, tag=tag or name, align_bytes=64)
+
+        lists = {}
+
+        def load_lists(*names):
+            for name in names:
+                lists[name] = held.tile(list(dram_lists[name].shape), U16, name="list_" + name)
+                nc.sync.dma_start(lists[name][:], dram_lists[name])
+
+        def load_scale_table(name, dram, cols):
+            table = tile(name, [P, cols], U8)
+            rows = dram[0].bitcast(I32)
+            nc.sync.dma_start(table[:].bitcast(I32), rows.unsqueeze(1).broadcast_to([16, 8, cols // 4]))
+            return table
+
+        def load_word_table(name, dram, cols):
+            table = tile(name, [P, cols], U32)
+            nc.sync.dma_start(table[:].bitcast(I32), dram[0].rearrange("p n t -> p (n t)").bitcast(I32))
+            return table
+
+        xs_table = load_scale_table("xs_table", x_scales, T_COLS)
+        load_lists("offs", "two", "hz", "duo")
+        ds_table = load_scale_table("ds_table", d_scales, G_COLS)
+        load_lists("k1", "k2", "k3")
+        dw_table = load_word_table("dw_table", d_words, G_COLS)
+        xw_table = load_word_table("xw_table", x_words, T_COLS)
+        load_lists("k4", "k5", "n1", "n2", "n3", "n4", "n5", "n6", "n7", "n8", "n9")
+        gs_raw = tile("gs_raw", [P, PACK], F32)
+        nc.sync.dma_start(gs_raw[:], gs.rearrange("(p t) o -> p (t o)", t=PACK))
+        gain = tile("gain", [P, PACK], F32)
+        nc.scalar.activation(gain[:], gs_raw[:], COPY, scale=SIXTEENTH)
+        ident = tile("ident", [P, P], F32)
+        make_identity(nc, ident[:])
+
+        def gather_scales(name, table, names):
+            picked = tile(name, [P, len(names) * S], U8)
+            for a, list_name in enumerate(names):
+                nc.vector.tensor_copy(picked[:, a * S : (a + 1) * S], table[:].indirect(lists[list_name][:]))
+            return picked
+
+        def place_scale_rows(name, picked, names):
+            placed = tile(name, [P, len(names) * S], U8)
+            nc.gpsimd.memset(placed[:].bitcast(U32), 0)
+            for r in range(4):
+                nc.sync.dma_start(placed[r:P:32, :].bitcast(I32), picked[8 * r : P : 32, :].bitcast(I32))
+            return {list_name: placed[:, a * S : (a + 1) * S] for a, list_name in enumerate(names)}
+
+        def gather_words(table, list_name, tag=None):
+            picked = tile("w_" + list_name, [P, S], U32, tag)
+            nc.vector.tensor_copy(picked[:], table[:].indirect(lists[list_name][:]))
+            return picked
+
+        scales = {}
+        x_names, d_names = ("offs", "two", "hz", "duo"), ("k1", "k2", "k3")
+        scales.update(place_scale_rows("xs_placed", gather_scales("xs_picked", xs_table, x_names), x_names))
+        scales.update(place_scale_rows("ds_placed", gather_scales("ds_picked", ds_table, d_names), d_names))
+        words = {}
+        for name in d_names:
+            words[name] = gather_words(dw_table, name)
+        for name in ("offs", "two", "hz"):
+            words[name] = gather_words(xw_table, name)
+
+        pairs = (("offs", "k1"), ("two", "k2"), ("hz", "k3"))
+        banks = [psum.tile([P, S], F32, name="mx%d" % c) for c in range(4)]
+        for n, (x_name, d_name) in enumerate(pairs):
+            for c in range(4):
+                cols = slice(c * P, (c + 1) * P)
+                nc.tensor.matmul_mx(
+                    banks[c][:], lhsT=words[x_name][:, cols].bitcast(FP8X4), lhsT_scale=scales[x_name][:, cols],
+                    rhs=words[d_name][:].bitcast(FP8X4), rhs_scale=scales[d_name],
+                    start=(n == 0), stop=(n == len(pairs) - 1),
+                )
+        h_rows = []
+        for t in range(PACK):
+            staged = tile("staged%d" % t, [P, 4, P], F32)
+            back = psum.tile([P, S], F32, name="tr%d" % t)
+            for c in range(4):
+                nc.scalar.activation(staged[:, c, :], banks[c][:].rearrange("j (p t) -> j t p", t=PACK)[:, t, :], COPY)
+                nc.tensor.transpose(back[:, c * P : (c + 1) * P], staged[:, c, :], ident[:])
+            h_t = tile("h%d" % t, [P, S], F32)
+            nc.scalar.activation(h_t[:], back[:], COPY)
+            pa = tile("pa%d" % t, [P, HALF], F32)
+            pb = tile("pb%d" % t, [P, HALF], F32)
+            nc.scalar.activation(pa[:], h_t[:].indirect(lists["n1"][:]), COPY)
+            nc.scalar.activation(pb[:], h_t[:].indirect(lists["n2"][:]), COPY)
+            h_rows.append((pa, pb))
+
+        late = ("k4", "k5")
+        late_picked = gather_scales("late_picked", ds_table, late)
+        late_dealt = tile("late_dealt", [P, len(late) * S], U8)
+        nc.vector.tensor_copy(
+            late_dealt[:].rearrange("p (a t c i) -> p a c t i", a=2, t=PACK, i=16),
+            late_picked[:].rearrange("p (a c i t) -> p a c t i", a=2, t=PACK, i=16),
+        )
+        scales.update(place_scale_rows("late_placed", late_dealt, late))
+        for name in late:
+            picked = gather_words(dw_table, name)
+            words[name] = tile("dealt_" + name, [P, S], U32)
+            nc.vector.tensor_copy(
+                words[name][:].rearrange("p (t c i) -> p c t i", t=PACK, i=4),
+                picked[:].rearrange("p (c i t) -> p c t i", t=PACK, i=4),
+            )
+
+        z_grouped = [tile("z_grouped%d" % u, [P, HALF, PACK], BF16) for u in range(2)]
+        for t in range(PACK):
+            pa, pb = h_rows[t]
+            ra = tile("ra%d" % t, [P, HALF], F32)
+            ub = tile("ub%d" % t, [P, S], F32)
+            sent = tile("sent%d" % t, [P, 2 * S], F32)
+            nc.vector.tensor_tensor(ra[:], pa[:], pb[:], ALU.min)
+            nc.vector.tensor_tensor(ub[:].indirect(lists["n4"][:]), pa[:], pb[:], ALU.add)
+            nc.vector.tensor_copy(ub[:].indirect(lists["n3"][:]), ra[:])
+            nc.vector.tensor_copy(sent[:].indirect(lists["n5"][:]), ub[:])
+            for u in range(2):
+                cols = slice(u * HALF, (u + 1) * HALF)
+                diff = tile("diff%d_%d" % (t, u), [P, HALF], F32)
+                nc.vector.tensor_tensor(diff[:], ub[:, cols], sent[:, cols], ALU.subtract)
+                nc.scalar.activation(z_grouped[u][:, :, t], diff[:], COPY, scale=gain[:, t : t + 1])
+
+        words["duo"] = gather_words(xw_table, "duo", tag="ub%d" % (PACK - 1))
+        z_codes, z_scales = [], []
+        for u in range(2):
+            codes = tile("z_codes%d" % u, [P, HALF], U32)
+            plane = tile("z_plane%d" % u, [P, HALF], U8)
+            nc.vector.quantize_mx(codes[:].bitcast(FP8X4), plane[:], z_grouped[u][:].rearrange("p j t -> p (j t)"))
+            z_codes.append(codes)
+            z_scales.append(plane)
+
+        out_grouped = [tile("out_grouped%d" % u, [P, HALF, PACK], BF16) for u in range(2)]
+        out_rows = out_0.rearrange("(p t) j -> t p j", t=PACK)
+        for t in range(PACK):
+            rows = slice(t * P, (t + 1) * P)
+            h2 = tile("h2_%d" % t, [P, S], F32)
+            for u in range(2):
+                cols = slice(u * HALF, (u + 1) * HALF)
+                bank = psum.tile([P, HALF], F32, name="second%d_%d" % (t, u), tag=("mx%d", "tr%d")[u] % t)
+                nc.tensor.matmul_mx(
+                    bank[:], lhsT=words["k5"][:, rows].bitcast(FP8X4), lhsT_scale=scales["k5"][:, rows],
+                    rhs=words["duo"][:, cols].bitcast(FP8X4), rhs_scale=scales["duo"][:, cols], start=True, stop=False,
+                )
+                nc.tensor.matmul_mx(
+                    bank[:], lhsT=words["k4"][:, rows].bitcast(FP8X4), lhsT_scale=scales["k4"][:, rows],
+                    rhs=z_codes[u][:].bitcast(FP8X4), rhs_scale=z_scales[u][:], start=False, stop=True,
+                )
+                nc.scalar.activation(h2[:, cols], bank[:], COPY, scale=SIXTEENTH)
+            pa2 = tile("pa2_%d" % t, [P, HALF], F32)
+            nb2 = tile("nb2_%d" % t, [P, HALF], F32)
+            ra2 = tile("ra2_%d" % t, [P, HALF], F32)
+            res = tile("res%d" % t, [P, S], F32)
+            pieces = 2 if t == 0 else 1
+            n = HALF // pieces
+            for s in range(pieces):
+                ent, col = slice(s * n, (s + 1) * n), slice(s * n // 16, (s + 1) * n // 16)
+                nc.scalar.activation(pa2[:, ent], h2[:].indirect(lists["n6"][:, col]), COPY)
+                nc.scalar.activation(nb2[:, ent], h2[:].indirect(lists["n7"][:, col]), COPY, scale=-1.0)
+                nc.vector.tensor_tensor(res[:].indirect(lists["n9"][:, col]), pa2[:, ent], nb2[:, ent], ALU.add)
+            nc.vector.scalar_tensor_tensor(ra2[:], nb2[:], -1.0, pa2[:], ALU.mult, ALU.max)
+            nc.vector.tensor_copy(res[:].indirect(lists["n8"][:]), ra2[:])
+            nc.sync.dma_start(out_rows[t], res[:])
+            for u in range(2):
+                nc.scalar.activation(out_grouped[u][:, :, t], res[:, u * HALF : (u + 1) * HALF], COPY)
+
+        out_plane = tile("out_plane", [P, S], U8)
+        out_words = out_1[0].rearrange("p n t -> p (n t)").bitcast(I32)
+        for u in range(2):
+            cols = slice(u * HALF, (u + 1) * HALF)
+            codes = tile("out_codes%d" % u, [P, HALF], U32)
+            nc.vector.quantize_mx(codes[:].bitcast(FP8X4), out_plane[:, cols], out_grouped[u][:].rearrange("p j t -> p (j t)"))
+            nc.sync.dma_start(out_words[:, cols], codes[:].bitcast(I32))
+        for q in range(4):
+            queue = (nc.sync, nc.scalar)[q % 2]
+            queue.dma_start(out_2[0][4 * q : 4 * q + 4, :].bitcast(I32), out_plane[32 * q : 32 * q + 4, :].bitcast(I32))

@@ -12,6 +12,7 @@ U8 = mybir.dt.uint8
 FP8X4 = mybir.dt.float8_e4m3fn_x4
 ALU = mybir.AluOpType
 COPY = mybir.ActivationFunctionType.Copy
+RELU = mybir.ActivationFunctionType.Relu
 
 P = 128
 PACK = 4
@@ -57,12 +58,12 @@ def tile_picked_mtthzmtcpsdcpmx_none_po_kernel(
             return table
 
         xs_table = load_scale_table("xs_table", x_scales, T_COLS)
-        load_lists("offs", "two", "hz", "duo")
+        load_lists("offs", "two", "hz")
         ds_table = load_scale_table("ds_table", d_scales, G_COLS)
         load_lists("k1", "k2", "k3")
-        dw_table = load_word_table("dw_table", d_words, G_COLS)
         xw_table = load_word_table("xw_table", x_words, T_COLS)
-        load_lists("k4", "k5", "n1", "n2", "n3", "n4", "n5", "n6", "n7", "n8", "n9")
+        dw_table = load_word_table("dw_table", d_words, G_COLS)
+        load_lists("duo", "k4", "k5", "n1", "n2", "n3", "n4", "n5", "n6", "n7", "n8", "n9")
         gs_raw = tile("gs_raw", [P, PACK], F32)
         nc.sync.dma_start(gs_raw[:], gs.rearrange("(p t) o -> p (t o)", t=PACK))
         gain = tile("gain", [P, PACK], F32)
@@ -70,8 +71,8 @@ def tile_picked_mtthzmtcpsdcpmx_none_po_kernel(
         ident = tile("ident", [P, P], F32)
         make_identity(nc, ident[:])
 
-        def gather_scales(name, table, names):
-            picked = tile(name, [P, len(names) * S], U8)
+        def gather_scales(name, table, names, tag=None):
+            picked = tile(name, [P, len(names) * S], U8, tag)
             for a, list_name in enumerate(names):
                 nc.vector.tensor_copy(picked[:, a * S : (a + 1) * S], table[:].indirect(lists[list_name][:]))
             return picked
@@ -83,20 +84,22 @@ def tile_picked_mtthzmtcpsdcpmx_none_po_kernel(
                 nc.sync.dma_start(placed[r:P:32, :].bitcast(I32), picked[8 * r : P : 32, :].bitcast(I32))
             return {list_name: placed[:, a * S : (a + 1) * S] for a, list_name in enumerate(names)}
 
-        def gather_words(table, list_name, tag=None):
+        def gather_words(table, list_name, tag=None, pieces=1):
             picked = tile("w_" + list_name, [P, S], U32, tag)
-            nc.vector.tensor_copy(picked[:], table[:].indirect(lists[list_name][:]))
+            n = S // pieces
+            for first in range(0, S, n):
+                offsets = lists[list_name][:, first // 16 : (first + n) // 16]
+                nc.vector.tensor_copy(picked[:, first : first + n], table[:].indirect(offsets))
             return picked
 
         scales = {}
-        x_names, d_names = ("offs", "two", "hz", "duo"), ("k1", "k2", "k3")
+        x_names, d_names = ("offs", "two", "hz"), ("k1", "k2", "k3")
         scales.update(place_scale_rows("xs_placed", gather_scales("xs_picked", xs_table, x_names), x_names))
         scales.update(place_scale_rows("ds_placed", gather_scales("ds_picked", ds_table, d_names), d_names))
         words = {}
-        for name in d_names:
-            words[name] = gather_words(dw_table, name)
-        for name in ("offs", "two", "hz"):
-            words[name] = gather_words(xw_table, name)
+        for x_name, d_name, tag in (("offs", "k1", None), ("two", "k2", "xs_picked"), ("hz", "k3", "ds_picked")):
+            words[d_name] = gather_words(dw_table, d_name)
+            words[x_name] = gather_words(xw_table, x_name, tag, 2 if x_name == "hz" else 1)
 
         pairs = (("offs", "k1"), ("two", "k2"), ("hz", "k3"))
         banks = [psum.tile([P, S], F32, name="mx%d" % c) for c in range(4)]
@@ -108,7 +111,25 @@ def tile_picked_mtthzmtcpsdcpmx_none_po_kernel(
                     rhs=words[d_name][:].bitcast(FP8X4), rhs_scale=scales[d_name],
                     start=(n == 0), stop=(n == len(pairs) - 1),
                 )
-        h_rows = []
+
+        def excess(name, first, second, sign_in, sign_out, bank_tag):
+            across = psum.tile([P, 2, P], F32, name=name + "_across", tag=bank_tag)
+            for c in range(2):
+                cols = slice(c * P, (c + 1) * P)
+                nc.tensor.matmul(across[:, c, :], first[:, cols], ident[:], is_transpose=True, start=True, stop=False)
+                nc.tensor.matmul(across[:, c, :], second[:, cols], ident[:], is_transpose=True, start=False, stop=True)
+            clipped = tile(name + "_clipped", [P, 2, P], F32)
+            nc.scalar.activation(clipped[:], across[:], RELU, scale=sign_in)
+            back = psum.tile([P, HALF], F32, name=name + "_back", tag=bank_tag)
+            for c in range(2):
+                nc.tensor.transpose(back[:, c * P : (c + 1) * P], clipped[:, c, :], ident[:])
+            result = tile(name, [P, HALF], F32)
+            nc.scalar.activation(result[:], back[:], COPY, scale=sign_out)
+            return result
+
+        pa = [tile("pa%d" % t, [P, HALF], F32) for t in range(PACK)]
+        pb = [tile("pb%d" % t, [P, HALF], F32) for t in range(PACK)]
+        cut = []
         for t in range(PACK):
             staged = tile("staged%d" % t, [P, 4, P], F32)
             back = psum.tile([P, S], F32, name="tr%d" % t)
@@ -117,45 +138,90 @@ def tile_picked_mtthzmtcpsdcpmx_none_po_kernel(
                 nc.tensor.transpose(back[:, c * P : (c + 1) * P], staged[:, c, :], ident[:])
             h_t = tile("h%d" % t, [P, S], F32)
             nc.scalar.activation(h_t[:], back[:], COPY)
-            pa = tile("pa%d" % t, [P, HALF], F32)
-            pb = tile("pb%d" % t, [P, HALF], F32)
-            nc.scalar.activation(pa[:], h_t[:].indirect(lists["n1"][:]), COPY)
-            nc.scalar.activation(pb[:], h_t[:].indirect(lists["n2"][:]), COPY)
-            h_rows.append((pa, pb))
+            nc.scalar.activation(pb[t][:], h_t[:].indirect(lists["n2"][:]), COPY)
+            nc.scalar.activation(pa[t][:], h_t[:].indirect(lists["n1"][:]), COPY)
+            nb = tile("nb%d" % t, [P, HALF], F32)
+            nc.scalar.activation(nb[:], pb[t][:], COPY, scale=-1.0)
+            cut.append(excess("cut%d" % t, pa[t], nb, 1.0, -1.0, "tr%d" % t))
 
         late = ("k4", "k5")
-        late_picked = gather_scales("late_picked", ds_table, late)
-        late_dealt = tile("late_dealt", [P, len(late) * S], U8)
+        late_picked = gather_scales("late_picked", ds_table, late, "w_k2")
+        late_packed = tile("late_packed", [P, S], U8)
+        nc.gpsimd.memset(late_packed[:].bitcast(U32), 0)
+        for a in range(len(late)):
+            for r in range(4):
+                nc.sync.dma_start(
+                    late_packed[4 * a + r : P : 32, :].bitcast(I32),
+                    late_picked[8 * r : P : 32, a * S : (a + 1) * S].bitcast(I32),
+                )
+        late_dealt = tile("late_dealt", [P, S], U8)
         nc.vector.tensor_copy(
-            late_dealt[:].rearrange("p (a t c i) -> p a c t i", a=2, t=PACK, i=16),
-            late_picked[:].rearrange("p (a c i t) -> p a c t i", a=2, t=PACK, i=16),
+            late_dealt[:].rearrange("p (t c i) -> p c t i", t=PACK, i=16),
+            late_packed[:].rearrange("p (c i t) -> p c t i", t=PACK, i=16),
         )
-        scales.update(place_scale_rows("late_placed", late_dealt, late))
-        for name in late:
-            picked = gather_words(dw_table, name)
-            words[name] = tile("dealt_" + name, [P, S], U32)
+        for a, name in enumerate(late):
+            scales[name] = late_dealt[4 * a :, :]
+
+        def deal_words(name, picked, first, count, tag=None):
+            dealt = tile(name, [P, count * P], U32, tag)
             nc.vector.tensor_copy(
-                words[name][:].rearrange("p (t c i) -> p c t i", t=PACK, i=4),
-                picked[:].rearrange("p (c i t) -> p c t i", t=PACK, i=4),
+                dealt[:].rearrange("p (t c i) -> p c t i", t=count, i=4),
+                picked[:].rearrange("p (c i t) -> p c t i", t=PACK, i=4)[:, :, first : first + count, :],
             )
+            return [dealt[:, t * P : (t + 1) * P] for t in range(count)]
+
+        scales.update(place_scale_rows("duo_placed", gather_scales("duo_picked", xs_table, ("duo",), "xs_picked"), ("duo",)))
+        words["duo"] = gather_words(xw_table, "duo", "w_offs")
+        k5_rows = deal_words("dealt_k5", gather_words(dw_table, "k5", "w_k1"), 0, PACK)
 
         z_grouped = [tile("z_grouped%d" % u, [P, HALF, PACK], BF16) for u in range(2)]
-        for t in range(PACK):
-            pa, pb = h_rows[t]
-            ra = tile("ra%d" % t, [P, HALF], F32)
-            ub = tile("ub%d" % t, [P, S], F32)
-            sent = tile("sent%d" % t, [P, 2 * S], F32)
-            nc.vector.tensor_tensor(ra[:], pa[:], pb[:], ALU.min)
-            nc.vector.tensor_tensor(ub[:].indirect(lists["n4"][:]), pa[:], pb[:], ALU.add)
-            nc.vector.tensor_copy(ub[:].indirect(lists["n3"][:]), ra[:])
-            nc.vector.tensor_copy(sent[:].indirect(lists["n5"][:]), ub[:])
+        minus_one = tile("minus_one", [P, S], F32)
+        nc.gpsimd.memset(minus_one[:], -1.0)
+        ub = [tile("ub%d" % t, [P, S], F32) for t in range(PACK)]
+
+        def put_sums(t):
+            nc.vector.tensor_tensor(ub[t][:].indirect(lists["n4"][:]), pa[t][:], pb[t][:], ALU.add)
+
+        def put_minima(t):
+            nc.vector.tensor_tensor(ub[t][:].indirect(lists["n3"][:]), pa[t][:], cut[t][:], ALU.add)
+
+        def send_on(t, tag=None):
+            sent = tile("sent%d" % t, [P, 2 * S], F32, tag)
+            nc.vector.tensor_tensor(sent[:].indirect(lists["n5"][:]), ub[t][:], minus_one[:], ALU.mult)
+            return sent
+
+        def weigh(t, u, diff):
+            nc.scalar.activation(z_grouped[u][:, :, t], diff, COPY, scale=gain[:, t : t + 1])
+
+        def add_on_tensor_engine(t, sent):
+            for u in range(2):
+                across = psum.tile([P, 2, P], F32, name="across%d_%d" % (t, u), tag=("tr3", "mx1")[u])
+                for c in range(2):
+                    cols = slice(u * HALF + c * P, u * HALF + (c + 1) * P)
+                    nc.tensor.matmul(across[:, c, :], ub[t][:, cols], ident[:], is_transpose=True, start=True, stop=False)
+                    nc.tensor.matmul(across[:, c, :], sent[:, cols], ident[:], is_transpose=True, start=False, stop=True)
+                summed = tile("summed%d_%d" % (t, u), [P, 2, P], F32)
+                nc.scalar.activation(summed[:], across[:], COPY)
+                back = psum.tile([P, HALF], F32, name="zback%d_%d" % (t, u), tag=("tr1", "tr2")[u])
+                for c in range(2):
+                    nc.tensor.transpose(back[:, c * P : (c + 1) * P], summed[:, c, :], ident[:])
+                weigh(t, u, back[:])
+
+        def add_on_vector(t, sent):
+            diff = tile("diff", [P, S], F32, "summed%d_1" % (t - 1))
             for u in range(2):
                 cols = slice(u * HALF, (u + 1) * HALF)
-                diff = tile("diff%d_%d" % (t, u), [P, HALF], F32)
-                nc.vector.tensor_tensor(diff[:], ub[:, cols], sent[:, cols], ALU.subtract)
-                nc.scalar.activation(z_grouped[u][:, :, t], diff[:], COPY, scale=gain[:, t : t + 1])
+                nc.vector.tensor_tensor(diff[:, cols], ub[t][:, cols], sent[:, cols], ALU.add)
+                weigh(t, u, diff[:, cols])
 
-        words["duo"] = gather_words(xw_table, "duo", tag="ub%d" % (PACK - 1))
+        for t in range(PACK):
+            put_sums(t)
+            if t > 0:
+                add_on_tensor_engine(t - 1, send_on(t - 1, "h%d" % t))
+            put_minima(t)
+        add_on_vector(PACK - 1, send_on(PACK - 1))
+
+        picked_k4 = gather_words(dw_table, "k4", "ub%d" % (PACK - 1))
         z_codes, z_scales = [], []
         for u in range(2):
             codes = tile("z_codes%d" % u, [P, HALF], U32)
@@ -163,40 +229,68 @@ def tile_picked_mtthzmtcpsdcpmx_none_po_kernel(
             nc.vector.quantize_mx(codes[:].bitcast(FP8X4), plane[:], z_grouped[u][:].rearrange("p j t -> p (j t)"))
             z_codes.append(codes)
             z_scales.append(plane)
+            if u == 0:
+                k4_rows = deal_words("dealt_k4_first", picked_k4, 0, 1)
+        k4_rows = k4_rows + deal_words("dealt_k4_rest", picked_k4, 1, PACK - 1, "z_grouped1")
 
-        out_grouped = [tile("out_grouped%d" % u, [P, HALF, PACK], BF16) for u in range(2)]
         out_rows = out_0.rearrange("(p t) j -> t p j", t=PACK)
-        for t in range(PACK):
+        pa2 = [tile("pa2_%d" % t, [P, HALF], F32) for t in range(PACK)]
+        nb2 = [tile("nb2_%d" % t, [P, HALF], F32) for t in range(PACK)]
+        res = [tile("res%d" % t, [P, S], F32) for t in range(PACK)]
+
+        def second_product(t):
             rows = slice(t * P, (t + 1) * P)
             h2 = tile("h2_%d" % t, [P, S], F32)
             for u in range(2):
                 cols = slice(u * HALF, (u + 1) * HALF)
-                bank = psum.tile([P, HALF], F32, name="second%d_%d" % (t, u), tag=("mx%d", "tr%d")[u] % t)
+                bank = psum.tile([P, HALF], F32, name="second%d_%d" % (t, u), tag=(("mx0", "tr0"), ("mx3", "mx2"))[t % 2][u])
                 nc.tensor.matmul_mx(
-                    bank[:], lhsT=words["k5"][:, rows].bitcast(FP8X4), lhsT_scale=scales["k5"][:, rows],
+                    bank[:], lhsT=k5_rows[t].bitcast(FP8X4), lhsT_scale=scales["k5"][:, rows],
                     rhs=words["duo"][:, cols].bitcast(FP8X4), rhs_scale=scales["duo"][:, cols], start=True, stop=False,
                 )
                 nc.tensor.matmul_mx(
-                    bank[:], lhsT=words["k4"][:, rows].bitcast(FP8X4), lhsT_scale=scales["k4"][:, rows],
+                    bank[:], lhsT=k4_rows[t].bitcast(FP8X4), lhsT_scale=scales["k4"][:, rows],
                     rhs=z_codes[u][:].bitcast(FP8X4), rhs_scale=z_scales[u][:], start=False, stop=True,
                 )
-                nc.scalar.activation(h2[:, cols], bank[:], COPY, scale=SIXTEENTH)
-            pa2 = tile("pa2_%d" % t, [P, HALF], F32)
-            nb2 = tile("nb2_%d" % t, [P, HALF], F32)
-            ra2 = tile("ra2_%d" % t, [P, HALF], F32)
-            res = tile("res%d" % t, [P, S], F32)
-            pieces = 2 if t == 0 else 1
-            n = HALF // pieces
-            for s in range(pieces):
-                ent, col = slice(s * n, (s + 1) * n), slice(s * n // 16, (s + 1) * n // 16)
-                nc.scalar.activation(pa2[:, ent], h2[:].indirect(lists["n6"][:, col]), COPY)
-                nc.scalar.activation(nb2[:, ent], h2[:].indirect(lists["n7"][:, col]), COPY, scale=-1.0)
-                nc.vector.tensor_tensor(res[:].indirect(lists["n9"][:, col]), pa2[:, ent], nb2[:, ent], ALU.add)
-            nc.vector.scalar_tensor_tensor(ra2[:], nb2[:], -1.0, pa2[:], ALU.mult, ALU.max)
-            nc.vector.tensor_copy(res[:].indirect(lists["n8"][:]), ra2[:])
-            nc.sync.dma_start(out_rows[t], res[:])
+                if t < 2 and (t, u) != (0, 0):
+                    nc.vector.tensor_scalar_mul(h2[:, cols], bank[:], SIXTEENTH)
+                else:
+                    nc.scalar.activation(h2[:, cols], bank[:], COPY, scale=SIXTEENTH)
+            return h2
+
+        def fetch_pairs(t, h2, first, n):
+            ent, col = slice(first, first + n), slice(first // 16, (first + n) // 16)
+            nc.scalar.activation(pa2[t][:, ent], h2[:].indirect(lists["n6"][:, col]), COPY)
+            nc.scalar.activation(nb2[t][:, ent], h2[:].indirect(lists["n7"][:, col]), COPY, scale=-1.0)
+
+        def put_differences(t, first, n):
+            ent, col = slice(first, first + n), slice(first // 16, (first + n) // 16)
+            nc.vector.tensor_tensor(
+                res[t][:].indirect(lists["n9"][:, col]), pa2[t][:, ent], nb2[t][:, ent], ALU.add
+            )
+
+        def put_maxima(t):
+            rise = excess("rise%d" % t, pa2[t], nb2[t], -1.0, 1.0, ("mx1", "tr1", "tr3", "tr2")[t])
+            nc.vector.tensor_tensor(res[t][:].indirect(lists["n8"][:]), pa2[t][:], rise[:], ALU.add)
+            nc.sync.dma_start(out_rows[t], res[t][:])
+
+        h2 = [second_product(0), second_product(1)]
+        for first in range(0, HALF, HALF // 2):
+            fetch_pairs(0, h2[0], first, HALF // 2)
+            put_differences(0, first, HALF // 2)
+        for t in range(1, PACK):
+            fetch_pairs(t, h2[1] if t == 1 else second_product(t), 0, HALF)
+            put_differences(t, 0, HALF)
+            put_maxima(t - 1)
+        put_maxima(PACK - 1)
+        out_grouped = [tile("out_grouped%d" % u, [P, HALF, PACK], BF16, "rise%d_clipped" % (3 - u)) for u in range(2)]
+        for t in range(PACK):
             for u in range(2):
-                nc.scalar.activation(out_grouped[u][:, :, t], res[:, u * HALF : (u + 1) * HALF], COPY)
+                cols = slice(u * HALF, (u + 1) * HALF)
+                if t >= 2 and u == 1:
+                    nc.vector.tensor_copy(out_grouped[u][:, :, t], res[t][:, cols])
+                else:
+                    nc.scalar.activation(out_grouped[u][:, :, t], res[t][:, cols], COPY)
 
         out_plane = tile("out_plane", [P, S], U8)
         out_words = out_1[0].rearrange("p n t -> p (n t)").bitcast(I32)

from contextlib import ExitStack

import concourse.mybir as mybir
from concourse.masks import make_identity

F32 = mybir.dt.float32
BF16 = mybir.dt.bfloat16
I32 = mybir.dt.int32
U32 = mybir.dt.uint32
U16 = mybir.dt.uint16
U8 = mybir.dt.uint8
FP8X4 = mybir.dt.float8_e4m3fn_x4
ALU = mybir.AluOpType
COPY = mybir.ActivationFunctionType.Copy
RELU = mybir.ActivationFunctionType.Relu

P = 128
PACK = 4
S = 512
HALF = S // 2
T_COLS, G_COLS = 1024, 2048
SIXTEENTH = 0.0625
FLOPS = 5 * 2 * 512 * 512 * 512


def tile_picked_mtthzmtcpsdcpmx_none_po_kernel(
    tc, x_words, x_scales, d_words, d_scales, gs, offs, k1, two, k2, hz, k3, n1, n2, n3, n4, n5, k4, k5, duo,
    n6, n7, n8, n9, out_0, out_1, out_2,
):
    nc = tc.nc
    dram_lists = dict(offs=offs, k1=k1, two=two, k2=k2, hz=hz, k3=k3, n1=n1, n2=n2, n3=n3, n4=n4, n5=n5,
                      k4=k4, k5=k5, duo=duo, n6=n6, n7=n7, n8=n8, n9=n9)

    with ExitStack() as ctx:
        held = ctx.enter_context(tc.tile_pool(name="held", bufs=1))
        sb = ctx.enter_context(tc.tile_pool(name="sb", bufs=1))
        psum = ctx.enter_context(tc.psum_pool(name="psum", bufs=1))

        def tile(name, shape, dtype, tag=None):
            return sb.tile(shape, dtype, name=name, tag=tag or name, align_bytes=64)

        lists = {}

        def load_lists(*names):
            for name in names:
                lists[name] = held.tile(list(dram_lists[name].shape), U16, name="list_" + name)
                nc.sync.dma_start(lists[name][:], dram_lists[name])

        def load_scale_table(name, dram, cols):
            table = tile(name, [P, cols], U8)
            rows = dram[0].bitcast(I32)
            nc.sync.dma_start(table[:].bitcast(I32), rows.unsqueeze(1).broadcast_to([16, 8, cols // 4]))
            return table

        def load_word_table(name, dram, cols):
            table = tile(name, [P, cols], U32)
            nc.sync.dma_start(table[:].bitcast(I32), dram[0].rearrange("p n t -> p (n t)").bitcast(I32))
            return table

        xs_table = load_scale_table("xs_table", x_scales, T_COLS)
        load_lists("offs", "two", "hz")
        ds_table = load_scale_table("ds_table", d_scales, G_COLS)
        load_lists("k1", "k2", "k3")
        xw_table = load_word_table("xw_table", x_words, T_COLS)
        dw_table = load_word_table("dw_table", d_words, G_COLS)
        load_lists("duo", "k4", "k5", "n1", "n2", "n3", "n4", "n5", "n6", "n7", "n8", "n9")
        gs_raw = tile("gs_raw", [P, PACK], F32)
        nc.sync.dma_start(gs_raw[:], gs.rearrange("(p t) o -> p (t o)", t=PACK))
        gain = tile("gain", [P, PACK], F32)
        nc.scalar.activation(gain[:], gs_raw[:], COPY, scale=SIXTEENTH)
        ident = tile("ident", [P, P], F32)
        make_identity(nc, ident[:])

        def gather_scales(name, table, names, tag=None):
            picked = tile(name, [P, len(names) * S], U8, tag)
            for a, list_name in enumerate(names):
                nc.vector.tensor_copy(picked[:, a * S : (a + 1) * S], table[:].indirect(lists[list_name][:]))
            return picked

        def place_scale_rows(name, picked, names):
            placed = tile(name, [P, len(names) * S], U8)
            nc.gpsimd.memset(placed[:].bitcast(U32), 0)
            for r in range(4):
                nc.sync.dma_start(placed[r:P:32, :].bitcast(I32), picked[8 * r : P : 32, :].bitcast(I32))
            return {list_name: placed[:, a * S : (a + 1) * S] for a, list_name in enumerate(names)}

        def gather_words(table, list_name, tag=None, pieces=1):
            picked = tile("w_" + list_name, [P, S], U32, tag)
            n = S // pieces
            for first in range(0, S, n):
                offsets = lists[list_name][:, first // 16 : (first + n) // 16]
                nc.vector.tensor_copy(picked[:, first : first + n], table[:].indirect(offsets))
            return picked

        scales = {}
        x_names, d_names = ("offs", "two", "hz"), ("k1", "k2", "k3")
        scales.update(place_scale_rows("xs_placed", gather_scales("xs_picked", xs_table, x_names), x_names))
        scales.update(place_scale_rows("ds_placed", gather_scales("ds_picked", ds_table, d_names), d_names))
        words = {}
        for x_name, d_name, tag in (("offs", "k1", None), ("two", "k2", "xs_picked"), ("hz", "k3", "ds_picked")):
            words[d_name] = gather_words(dw_table, d_name)
            words[x_name] = gather_words(xw_table, x_name, tag, 2 if x_name == "hz" else 1)

        pairs = (("offs", "k1"), ("two", "k2"), ("hz", "k3"))
        banks = [psum.tile([P, S], F32, name="mx%d" % c) for c in range(4)]
        for n, (x_name, d_name) in enumerate(pairs):
            for c in range(4):
                cols = slice(c * P, (c + 1) * P)
                nc.tensor.matmul_mx(
                    banks[c][:], lhsT=words[x_name][:, cols].bitcast(FP8X4), lhsT_scale=scales[x_name][:, cols],
                    rhs=words[d_name][:].bitcast(FP8X4), rhs_scale=scales[d_name],
                    start=(n == 0), stop=(n == len(pairs) - 1),
                )

        def excess(name, first, second, sign_in, sign_out, bank_tag):
            across = psum.tile([P, 2, P], F32, name=name + "_across", tag=bank_tag)
            for c in range(2):
                cols = slice(c * P, (c + 1) * P)
                nc.tensor.matmul(across[:, c, :], first[:, cols], ident[:], is_transpose=True, start=True, stop=False)
                nc.tensor.matmul(across[:, c, :], second[:, cols], ident[:], is_transpose=True, start=False, stop=True)
            clipped = tile(name + "_clipped", [P, 2, P], F32)
            nc.scalar.activation(clipped[:], across[:], RELU, scale=sign_in)
            back = psum.tile([P, HALF], F32, name=name + "_back", tag=bank_tag)
            for c in range(2):
                nc.tensor.transpose(back[:, c * P : (c + 1) * P], clipped[:, c, :], ident[:])
            result = tile(name, [P, HALF], F32)
            nc.scalar.activation(result[:], back[:], COPY, scale=sign_out)
            return result

        pa = [tile("pa%d" % t, [P, HALF], F32) for t in range(PACK)]
        pb = [tile("pb%d" % t, [P, HALF], F32) for t in range(PACK)]
        cut = []
        for t in range(PACK):
            staged = tile("staged%d" % t, [P, 4, P], F32)
            back = psum.tile([P, S], F32, name="tr%d" % t)
            for c in range(4):
                nc.scalar.activation(staged[:, c, :], banks[c][:].rearrange("j (p t) -> j t p", t=PACK)[:, t, :], COPY)
                nc.tensor.transpose(back[:, c * P : (c + 1) * P], staged[:, c, :], ident[:])
            h_t = tile("h%d" % t, [P, S], F32)
            nc.scalar.activation(h_t[:], back[:], COPY)
            nc.scalar.activation(pb[t][:], h_t[:].indirect(lists["n2"][:]), COPY)
            nc.scalar.activation(pa[t][:], h_t[:].indirect(lists["n1"][:]), COPY)
            nb = tile("nb%d" % t, [P, HALF], F32)
            nc.scalar.activation(nb[:], pb[t][:], COPY, scale=-1.0)
            cut.append(excess("cut%d" % t, pa[t], nb, 1.0, -1.0, "tr%d" % t))

        late = ("k4", "k5")
        late_picked = gather_scales("late_picked", ds_table, late, "w_k2")
        late_packed = tile("late_packed", [P, S], U8)
        nc.gpsimd.memset(late_packed[:].bitcast(U32), 0)
        for a in range(len(late)):
            for r in range(4):
                nc.sync.dma_start(
                    late_packed[4 * a + r : P : 32, :].bitcast(I32),
                    late_picked[8 * r : P : 32, a * S : (a + 1) * S].bitcast(I32),
                )
        late_dealt = tile("late_dealt", [P, S], U8)
        nc.vector.tensor_copy(
            late_dealt[:].rearrange("p (t c i) -> p c t i", t=PACK, i=16),
            late_packed[:].rearrange("p (c i t) -> p c t i", t=PACK, i=16),
        )
        for a, name in enumerate(late):
            scales[name] = late_dealt[4 * a :, :]

        def deal_words(name, picked, first, count, tag=None):
            dealt = tile(name, [P, count * P], U32, tag)
            nc.vector.tensor_copy(
                dealt[:].rearrange("p (t c i) -> p c t i", t=count, i=4),
                picked[:].rearrange("p (c i t) -> p c t i", t=PACK, i=4)[:, :, first : first + count, :],
            )
            return [dealt[:, t * P : (t + 1) * P] for t in range(count)]

        scales.update(place_scale_rows("duo_placed", gather_scales("duo_picked", xs_table, ("duo",), "xs_picked"), ("duo",)))
        words["duo"] = gather_words(xw_table, "duo", "w_offs")
        k5_rows = deal_words("dealt_k5", gather_words(dw_table, "k5", "w_k1"), 0, PACK)

        z_grouped = [tile("z_grouped%d" % u, [P, HALF, PACK], BF16) for u in range(2)]
        minus_one = tile("minus_one", [P, S], F32)
        nc.gpsimd.memset(minus_one[:], -1.0)
        ub = [tile("ub%d" % t, [P, S], F32) for t in range(PACK)]

        def put_sums(t):
            nc.vector.tensor_tensor(ub[t][:].indirect(lists["n4"][:]), pa[t][:], pb[t][:], ALU.add)

        def put_minima(t):
            nc.vector.tensor_tensor(ub[t][:].indirect(lists["n3"][:]), pa[t][:], cut[t][:], ALU.add)

        def send_on(t, tag=None):
            sent = tile("sent%d" % t, [P, 2 * S], F32, tag)
            nc.vector.tensor_tensor(sent[:].indirect(lists["n5"][:]), ub[t][:], minus_one[:], ALU.mult)
            return sent

        def weigh(t, u, diff):
            nc.scalar.activation(z_grouped[u][:, :, t], diff, COPY, scale=gain[:, t : t + 1])

        def add_on_tensor_engine(t, sent):
            for u in range(2):
                across = psum.tile([P, 2, P], F32, name="across%d_%d" % (t, u), tag=("tr3", "mx1")[u])
                for c in range(2):
                    cols = slice(u * HALF + c * P, u * HALF + (c + 1) * P)
                    nc.tensor.matmul(across[:, c, :], ub[t][:, cols], ident[:], is_transpose=True, start=True, stop=False)
                    nc.tensor.matmul(across[:, c, :], sent[:, cols], ident[:], is_transpose=True, start=False, stop=True)
                summed = tile("summed%d_%d" % (t, u), [P, 2, P], F32)
                nc.scalar.activation(summed[:], across[:], COPY)
                back = psum.tile([P, HALF], F32, name="zback%d_%d" % (t, u), tag=("tr1", "tr2")[u])
                for c in range(2):
                    nc.tensor.transpose(back[:, c * P : (c + 1) * P], summed[:, c, :], ident[:])
                weigh(t, u, back[:])

        def add_on_vector(t, sent):
            diff = tile("diff", [P, S], F32, "summed%d_1" % (t - 1))
            for u in range(2):
                cols = slice(u * HALF, (u + 1) * HALF)
                nc.vector.tensor_tensor(diff[:, cols], ub[t][:, cols], sent[:, cols], ALU.add)
                weigh(t, u, diff[:, cols])

        for t in range(PACK):
            put_sums(t)
            if t > 0:
                add_on_tensor_engine(t - 1, send_on(t - 1, "h%d" % t))
            put_minima(t)
        add_on_vector(PACK - 1, send_on(PACK - 1))

        picked_k4 = gather_words(dw_table, "k4", "ub%d" % (PACK - 1))
        z_codes, z_scales = [], []
        for u in range(2):
            codes = tile("z_codes%d" % u, [P, HALF], U32)
            plane = tile("z_plane%d" % u, [P, HALF], U8)
            nc.vector.quantize_mx(codes[:].bitcast(FP8X4), plane[:], z_grouped[u][:].rearrange("p j t -> p (j t)"))
            z_codes.append(codes)
            z_scales.append(plane)
            if u == 0:
                k4_rows = deal_words("dealt_k4_first", picked_k4, 0, 1)
        k4_rows = k4_rows + deal_words("dealt_k4_rest", picked_k4, 1, PACK - 1, "z_grouped1")

        out_rows = out_0.rearrange("(p t) j -> t p j", t=PACK)
        pa2 = [tile("pa2_%d" % t, [P, HALF], F32) for t in range(PACK)]
        nb2 = [tile("nb2_%d" % t, [P, HALF], F32) for t in range(PACK)]
        res = [tile("res%d" % t, [P, S], F32) for t in range(PACK)]

        def second_product(t):
            rows = slice(t * P, (t + 1) * P)
            h2 = tile("h2_%d" % t, [P, S], F32)
            for u in range(2):
                cols = slice(u * HALF, (u + 1) * HALF)
                bank = psum.tile([P, HALF], F32, name="second%d_%d" % (t, u), tag=(("mx0", "tr0"), ("mx3", "mx2"))[t % 2][u])
                nc.tensor.matmul_mx(
                    bank[:], lhsT=k5_rows[t].bitcast(FP8X4), lhsT_scale=scales["k5"][:, rows],
                    rhs=words["duo"][:, cols].bitcast(FP8X4), rhs_scale=scales["duo"][:, cols], start=True, stop=False,
                )
                nc.tensor.matmul_mx(
                    bank[:], lhsT=k4_rows[t].bitcast(FP8X4), lhsT_scale=scales["k4"][:, rows],
                    rhs=z_codes[u][:].bitcast(FP8X4), rhs_scale=z_scales[u][:], start=False, stop=True,
                )
                if t < 2 and (t, u) != (0, 0):
                    nc.vector.tensor_scalar_mul(h2[:, cols], bank[:], SIXTEENTH)
                else:
                    nc.scalar.activation(h2[:, cols], bank[:], COPY, scale=SIXTEENTH)
            return h2

        def fetch_pairs(t, h2, first, n):
            ent, col = slice(first, first + n), slice(first // 16, (first + n) // 16)
            nc.scalar.activation(pa2[t][:, ent], h2[:].indirect(lists["n6"][:, col]), COPY)
            nc.scalar.activation(nb2[t][:, ent], h2[:].indirect(lists["n7"][:, col]), COPY, scale=-1.0)

        def put_differences(t, first, n):
            ent, col = slice(first, first + n), slice(first // 16, (first + n) // 16)
            nc.vector.tensor_tensor(
                res[t][:].indirect(lists["n9"][:, col]), pa2[t][:, ent], nb2[t][:, ent], ALU.add
            )

        def put_maxima(t):
            rise = excess("rise%d" % t, pa2[t], nb2[t], -1.0, 1.0, ("mx1", "tr1", "tr3", "tr2")[t])
            nc.vector.tensor_tensor(res[t][:].indirect(lists["n8"][:]), pa2[t][:], rise[:], ALU.add)
            nc.sync.dma_start(out_rows[t], res[t][:])

        h2 = [second_product(0), second_product(1)]
        for first in range(0, HALF, HALF // 2):
            fetch_pairs(0, h2[0], first, HALF // 2)
            put_differences(0, first, HALF // 2)
        for t in range(1, PACK):
            fetch_pairs(t, h2[1] if t == 1 else second_product(t), 0, HALF)
            put_differences(t, 0, HALF)
            put_maxima(t - 1)
        put_maxima(PACK - 1)
        out_grouped = [tile("out_grouped%d" % u, [P, HALF, PACK], BF16, "rise%d_clipped" % (3 - u)) for u in range(2)]
        for t in range(PACK):
            for u in range(2):
                cols = slice(u * HALF, (u + 1) * HALF)
                if t >= 2 and u == 1:
                    nc.vector.tensor_copy(out_grouped[u][:, :, t], res[t][:, cols])
                else:
                    nc.scalar.activation(out_grouped[u][:, :, t], res[t][:, cols], COPY)

        out_plane = tile("out_plane", [P, S], U8)
        out_words = out_1[0].rearrange("p n t -> p (n t)").bitcast(I32)
        for u in range(2):
            cols = slice(u * HALF, (u + 1) * HALF)
            codes = tile("out_codes%d" % u, [P, HALF], U32)
            nc.vector.quantize_mx(codes[:].bitcast(FP8X4), out_plane[:, cols], out_grouped[u][:].rearrange("p j t -> p (j t)"))
            nc.sync.dma_start(out_words[:, cols], codes[:].bitcast(I32))
        for q in range(4):
            queue = (nc.sync, nc.scalar)[q % 2]
            queue.dma_start(out_2[0][4 * q : 4 * q + 4, :].bitcast(I32), out_plane[32 * q : 32 * q + 4, :].bitcast(I32))
